import numpy as np
import ml_dtypes


def mxq(x, axis, fmt="e4m3"):
    dtype, down = {"e4m3": (ml_dtypes.float8_e4m3fn, 7), "e5m2": (ml_dtypes.float8_e5m2, 14)}[fmt]
    v = np.moveaxis(np.asarray(x, np.float32).astype(ml_dtypes.bfloat16).astype(np.float64), axis, -1)
    blocks = v.reshape(v.shape[:-1] + (-1, 32))
    amax = np.abs(blocks).max(-1, keepdims=True)
    byte = np.maximum(np.where(amax > 0, np.frexp(amax)[1] - 1 + 127, 0) - down, 1)
    scale = np.exp2(byte - 127.0)
    codes = (blocks / scale).astype(np.float32).astype(dtype).astype(np.float64)
    return np.moveaxis((codes * scale).reshape(v.shape), -1, axis)


WIDE = False


def mx_kscale(k):
    if not WIDE:
        return np.ones(k)
    levels = np.array([10, -10, 5, -5, 0])
    if k % 512:
        return np.exp2(np.random.permutation(np.resize(levels, k // 32))).repeat(32)
    a = np.empty((k // 512, 16))
    for p in range(k // 512):
        a[p, :8] = np.random.permutation(np.resize(levels, 8))
        for g in range(8):
            far = levels[np.abs(levels - a[p, g]) >= 10]
            a[p, g + 8] = far[np.random.randint(len(far))]
    return np.exp2(a.ravel()).repeat(32)


def f64(x):
    return np.asarray(x).astype(np.float64)


def striped(idx):
    return np.tile(np.asarray(idx).reshape(-1, 16).T, (8, 1)).astype(np.uint16)


def unstriped(offs):
    return offs[:16].T.reshape(-1).astype(np.int64)


E2M1 = np.array([0.0, 0.5, 1.0, 1.5, 2.0, 3.0, 4.0, 6.0, -0.0, -0.5, -1.0, -1.5, -2.0, -3.0, -4.0, -6.0])


def pack_weight(w, fmt):
    k, n = w.shape
    w = f64(np.asarray(w, np.float32).astype(ml_dtypes.bfloat16)).reshape(k // 32, 32, n)
    amax = np.abs(w).max(1)
    if fmt == "e4m3":
        byte = np.frexp(amax)[1] - 1 + 127 - 7
    else:
        mant, ex = np.frexp(amax / 6.0)
        byte = np.where(mant > 0.5, ex, ex - 1) + 127
    byte = np.clip(np.where(amax > 0, byte, 1), 1, 254)
    scaled = (w * np.exp2(127.0 - byte)[:, None, :]).reshape(k, n).astype(np.float32)
    by_word = np.ascontiguousarray(scaled.reshape(k // 512, 128, 4, n).transpose(0, 1, 3, 2))
    if fmt == "e4m3":
        words = by_word.astype(ml_dtypes.float8_e4m3fn).view(np.uint8)
    else:
        c = by_word.astype(ml_dtypes.float4_e2m1fn).view(np.uint8) & 0xF
        words = (c[..., 0::2] | (c[..., 1::2] << 4)).reshape(k // 512, 128, 2 * n)
    return np.ascontiguousarray(words), np.ascontiguousarray(byte.astype(np.uint8).reshape(k // 512, 16, n))


def unpack_weight(words, scales, fmt):
    g, _, n = scales.shape
    words = np.ascontiguousarray(words).reshape(g, 128, n, -1)
    if fmt == "e4m3":
        vals = words.view(ml_dtypes.float8_e4m3fn).astype(np.float64)
    else:
        nib = np.empty((g, 128, n, 4), np.uint8)
        nib[..., 0::2] = words & 0xF
        nib[..., 1::2] = words >> 4
        vals = E2M1[nib]
    vals = vals * np.repeat(np.exp2(scales.astype(np.float64) - 127.0), 8, axis=1)[..., None]
    return vals.transpose(0, 1, 3, 2).reshape(g * 512, n)


B, N, T, D, DV, NQ = 2, 512, 2048, 512, 512, 128
PAGE = 32


def setup_inputs():
    n = np.random.standard_normal
    pages = np.random.permutation(T // PAGE)[:B * N // PAGE]
    idx = (pages[:, None] * PAGE + np.arange(PAGE)[None, :]).reshape(-1)
    s = mx_kscale(D)[:, None]
    u = np.ones(T)
    u[idx] = mx_kscale(B * N)
    r = np.random.uniform(0.5, 2.0, T)
    qp = [pack_weight(x, "e4m3") for x in n((B, D, NQ)) * s * (0.60 / np.sqrt(D))]
    k = n((D, T)) / s
    v = n((DV, T)) / (u * r)
    kp = pack_weight(k, "e4m3")
    return {
        "q_words": np.stack([x[0] for x in qp]),
        "q_scales": np.stack([x[1] for x in qp]),
        "k_words": kp[0],
        "k_scales": kp[1],
        "vT": v.astype(np.float32),
        "vs": np.tile(u * r, (128, 1)).astype(np.float32),
        "offs": striped(idx),
    }


def reference(q_words, q_scales, k_words, k_scales, vT, vs, offs):
    idx = unstriped(offs)
    k = unpack_weight(k_words, k_scales, "e4m3")
    v = f64(vT)
    pick = lambda x: x[:, idx].reshape(x.shape[0], B, N).transpose(1, 0, 2)
    q = np.stack([unpack_weight(q_words[b], q_scales[b], "e4m3") for b in range(B)])
    score = q.transpose(0, 2, 1) @ pick(k)
    m = score.max(-1, keepdims=True)
    p = np.exp(score - m)
    total = p.sum(-1, keepdims=True)
    w = p * pick(f64(vs))[:, :1, :]
    y = mxq(w, 2, "e4m3") @ mxq(pick(v).transpose(0, 2, 1), 1, "e4m3")
    y = y / total
    return y

@@ -1,0 +1,198 @@
+from contextlib import ExitStack
+
+import concourse.mybir as mybir
+from concourse.masks import make_identity
+
+B, N, T, D, DV, NQ = 2, 512, 2048, 512, 512, 128
+P = 128
+PACK = 4
+BLOCKS = DV // P
+SCALAR_BLOCKS = 1
+
+FLOPS = 2 * B * NQ * N * (D + DV)
+
+F32 = mybir.dt.float32
+BF16 = mybir.dt.bfloat16
+I32 = mybir.dt.int32
+U32 = mybir.dt.uint32
+U16 = mybir.dt.uint16
+U8 = mybir.dt.uint8
+FP8X4 = mybir.dt.float8_e4m3fn_x4
+ACT = mybir.ActivationFunctionType
+ALU = mybir.AluOpType
+AXIS = mybir.AxisListType
+
+
+def tile_attend_qpk_kernel(tc, q_words, q_scales, k_words, k_scales, vT, vs, offs, out):
+    nc = tc.nc
+    with ExitStack() as ctx:
+        sb = ctx.enter_context(tc.tile_pool(name="sb", bufs=1))
+        ps = ctx.enter_context(tc.psum_pool(name="ps", bufs=1))
+
+        offsets = sb.tile([P, B * N // 16], U16, name="offsets")
+        nc.sync.dma_start(offsets[:], offs)
+
+        def seq_offsets(b):
+            return offsets[:, b * (N // 16) : (b + 1) * (N // 16)]
+
+        def load_values(j, tag):
+            pool_tile = sb.tile([P, T], F32, name=f"v_pool{j}", tag=tag)
+            nc.sync.dma_start(pool_tile[:], vT[j * P : (j + 1) * P, :])
+            return pool_tile
+
+        v_pool = {0: load_values(0, "v0")}
+        kw_pool = sb.tile([P, T], U32, name="kw_pool")
+        nc.sync.dma_start(kw_pool[:].bitcast(I32), k_words[0].rearrange("g t r -> g (t r)").bitcast(I32))
+        v_pool[1] = load_values(1, "v1")
+
+        qw = sb.tile([P, B * NQ], U32, name="qw", align_bytes=64)
+        nc.scalar.dma_start(
+            qw[:].bitcast(I32).rearrange("g (b q) -> g b q", b=B),
+            q_words[:, 0].rearrange("b g q r -> g b (q r)").bitcast(I32),
+        )
+        vs_pool = sb.tile([P, T], F32, name="vs_pool", tag="v2")
+        nc.vector.memset(vs_pool[:], 0.0)
+        nc.scalar.dma_start(vs_pool[0:1, :], vs[0:1, :])
+        ks_pool = sb.tile([P, T], U8, name="ks_pool", tag="v3")
+        nc.vector.memset(ks_pool[:].bitcast(I32), 0)
+        for quad in range(4):
+            nc.scalar.dma_start(
+                ks_pool[32 * quad : 32 * quad + 4, :].bitcast(I32), k_scales[0, 4 * quad : 4 * quad + 4, :].bitcast(I32)
+            )
+        warm = sb.tile([P, 1], F32, name="warm")
+        warm_out = sb.tile([P, 1], F32, name="warm_out")
+        nc.vector.memset(warm[:], 0.0)
+        nc.scalar.activation(warm_out[:], warm[:], ACT.Exp)
+
+        qs = sb.tile([P, B * NQ], U8, name="qs", align_bytes=64)
+        ident = sb.tile([P, P], F32, name="ident")
+        make_identity(nc, ident[:])
+        nc.gpsimd.memset(qs[:].bitcast(I32), 0)
+        for quad in range(4):
+            nc.gpsimd.dma_start(
+                qs[32 * quad : 32 * quad + 4, :].bitcast(I32).rearrange("r (b w) -> r b w", b=B),
+                q_scales[:, 0, 4 * quad : 4 * quad + 4, :].bitcast(I32).rearrange("b r w -> r b w"),
+            )
+
+        vs_got = sb.tile([P, B * N], F32, name="vs_got")
+        nc.vector.tensor_copy(vs_got[:], vs_pool[:].indirect(offsets[:]))
+        ks_got = sb.tile([P, B * N], U8, name="ks_got", align_bytes=64)
+        nc.vector.tensor_copy(ks_got[:], ks_pool[:].indirect(offsets[:]))
+        v_pool[2] = load_values(2, "v2")
+        v_pool[3] = load_values(3, "v3")
+
+        def scalar_gather(j):
+            cast = sb.tile([P, T], BF16, name=f"v_cast{j}")
+            nc.scalar.activation(cast[:], v_pool[j][:], ACT.Copy)
+            got = sb.tile([P, B * N], BF16, name=f"v_got{j}")
+            nc.scalar.activation(got[:], cast[:].indirect(offsets[:]), ACT.Copy)
+            return got
+
+        def vector_gather(j, offsets_used, seqs, name):
+            got = sb.tile([P, seqs * N], BF16, name=name)
+            nc.vector.tensor_copy(got[:], v_pool[j][:].indirect(offsets_used))
+            return got
+
+        kw_got = []
+        for b in range(B):
+            kw_got.append(sb.tile([P, N], U32, name=f"kw_got{b}", align_bytes=64))
+            nc.vector.tensor_copy(kw_got[b][:], kw_pool[:].indirect(seq_offsets(b)))
+
+        vs_col = []
+        for b in range(B):
+            turned = ps.tile([P, PACK, P], F32, name=f"vs_turned{b}", tag=f"turn{b}")
+            for t in range(PACK):
+                nc.tensor.transpose(turned[:, t, :], vs_got[:, b * N + t : (b + 1) * N : PACK], ident[:])
+            vs_col.append(sb.tile([P, PACK], F32, name=f"vs_col{b}"))
+            nc.scalar.copy(vs_col[b][:], turned[:, :, 0])
+
+        got0 = scalar_gather(0) if SCALAR_BLOCKS > 0 else None
+
+        w_codes, w_scales, inv_sum = [], [], []
+        for b in range(B):
+            q_cols = slice(b * NQ, (b + 1) * NQ)
+            score = ps.tile([NQ, N], F32, name=f"score{b}")
+            nc.tensor.matmul_mx(
+                out=score[:],
+                lhsT=qw[:, q_cols].bitcast(FP8X4),
+                lhsT_scale=qs[:, q_cols],
+                rhs=kw_got[b][:].bitcast(FP8X4),
+                rhs_scale=ks_got[:, b * N : (b + 1) * N],
+                start=True,
+                stop=True,
+            )
+            neg_max = sb.tile([NQ, 1], F32, name=f"neg_max{b}")
+            nc.vector.tensor_reduce(neg_max[:], score[:], AXIS.X, ALU.max, negate=True)
+            prob = sb.tile([NQ, PACK, P], F32, name=f"prob{b}")
+            row_sum = sb.tile([NQ, 1], F32, name=f"row_sum{b}")
+            nc.scalar.activation(
+                prob[:], score[:].rearrange("q (s t) -> q t s", t=PACK), ACT.Exp, bias=neg_max[:], accum_out=row_sum[:]
+            )
+            prob_turned = ps.tile([P, PACK, NQ], F32, name=f"prob_turned{b}", tag=f"turn{b}")
+            for t in range(PACK):
+                nc.tensor.transpose(prob_turned[:, t, :], prob[:, t, :], ident[:])
+            weight = sb.tile([P, NQ, PACK], BF16, name=f"weight{b}", align_bytes=64)
+            nc.vector.tensor_tensor(
+                weight[:],
+                prob_turned[:].rearrange("s t q -> s q t"),
+                vs_col[b][:].unsqueeze(1).broadcast_to([P, NQ, PACK]),
+                ALU.mult,
+            )
+            inv_sum.append(sb.tile([NQ, 1], F32, name=f"inv_sum{b}"))
+            nc.vector.reciprocal(inv_sum[b][:], row_sum[:])
+            w_codes.append(sb.tile([P, NQ], U32, name=f"w_codes{b}", align_bytes=64))
+            w_scales.append(sb.tile([P, NQ], U8, name=f"w_scales{b}", align_bytes=64))
+            nc.vector.quantize_mx(
+                out=w_codes[b][:].bitcast(FP8X4), scales=w_scales[b][:], in_=weight[:].rearrange("s q t -> s (q t)")
+            )
+
+        acc = [ps.tile([NQ, DV], F32, name=f"acc{b}") for b in range(B)]
+        result = {}
+
+        def multiply(j, got, seqs, name, bank):
+            count = len(seqs)
+            words = got[:].bitcast(F32)
+            turned = ps.tile([P, count, 2, P], F32, name=f"v_turned{name}", tag=f"v_turn{bank}")
+            for i in range(count):
+                for u in range(2):
+                    nc.tensor.transpose(turned[:, i, u, :], words[:, i * (N // 2) + u : (i + 1) * (N // 2) : 2], ident[:])
+            woven = sb.tile([P, count * P * PACK], BF16, name=f"v_woven{name}", align_bytes=64)
+            nc.scalar.copy(
+                woven[:].bitcast(F32).rearrange("s (i e u) -> s i e u", i=count, u=2),
+                turned[:].rearrange("s i u e -> s i e u"),
+            )
+            codes = sb.tile([P, count * P], U32, name=f"v_codes{name}", align_bytes=64)
+            scales = sb.tile([P, count * P], U8, name=f"v_scales{name}", align_bytes=64)
+            nc.vector.quantize_mx(out=codes[:].bitcast(FP8X4), scales=scales[:], in_=woven[:])
+            e_cols = slice(j * P, (j + 1) * P)
+            for i, b in enumerate(seqs):
+                nc.tensor.matmul_mx(
+                    out=acc[b][:, e_cols],
+                    lhsT=w_codes[b][:].bitcast(FP8X4),
+                    lhsT_scale=w_scales[b][:],
+                    rhs=codes[:, i * P : (i + 1) * P].bitcast(FP8X4),
+                    rhs_scale=scales[:, i * P : (i + 1) * P],
+                    start=True,
+                    stop=True,
+                )
+
+        def store(b, first, last):
+            cols = slice(first * P, last * P)
+            staged = sb.tile([NQ, (last - first) * P], F32, name=f"staged{b}_{first}")
+            nc.scalar.activation(staged[:], acc[b][:, cols], ACT.Copy, scale=inv_sum[b][:])
+            nc.sync.dma_start(out[b, :, cols], staged[:])
+
+        for j in range(BLOCKS - 1):
+            if j == 0 and SCALAR_BLOCKS > 0:
+                got = got0
+            elif j < SCALAR_BLOCKS:
+                got = scalar_gather(j)
+            else:
+                got = vector_gather(j, offsets[:], B, f"v_got{j}")
+            multiply(j, got, list(range(B)), f"{j}", j % 2)
+        last_got = [vector_gather(BLOCKS - 1, seq_offsets(b), 1, f"v_got_last{b}") for b in range(B)]
+        for b in range(B):
+            store(b, 0, BLOCKS - 1)
+        for b in range(B):
+            multiply(BLOCKS - 1, last_got[b], [b], f"last{b}", (BLOCKS - 1 + b) % 2)
+            store(b, BLOCKS - 1, BLOCKS)

@@ -7,7 +7,7 @@ B, N, T, D, DV, NQ = 2, 512, 2048, 512, 512, 128
 P = 128
 PACK = 4
 BLOCKS = DV // P
-SCALAR_BLOCKS = 1
+SCALAR_BLOCKS = 2
 
 FLOPS = 2 * B * NQ * N * (D + DV)
 
@@ -45,39 +45,35 @@ def tile_attend_qpk_kernel(tc, q_words, q_scales, k_words, k_scales, vT, vs, off
         nc.sync.dma_start(kw_pool[:].bitcast(I32), k_words[0].rearrange("g t r -> g (t r)").bitcast(I32))
         v_pool[1] = load_values(1, "v1")
 
-        qw = sb.tile([P, B * NQ], U32, name="qw", align_bytes=64)
-        nc.scalar.dma_start(
-            qw[:].bitcast(I32).rearrange("g (b q) -> g b q", b=B),
-            q_words[:, 0].rearrange("b g q r -> g b (q r)").bitcast(I32),
-        )
-        vs_pool = sb.tile([P, T], F32, name="vs_pool", tag="v2")
-        nc.vector.memset(vs_pool[:], 0.0)
-        nc.scalar.dma_start(vs_pool[0:1, :], vs[0:1, :])
-        ks_pool = sb.tile([P, T], U8, name="ks_pool", tag="v3")
+        ks_pool = sb.tile([P, T], U8, name="ks_pool", tag="v2")
         nc.vector.memset(ks_pool[:].bitcast(I32), 0)
         for quad in range(4):
             nc.scalar.dma_start(
                 ks_pool[32 * quad : 32 * quad + 4, :].bitcast(I32), k_scales[0, 4 * quad : 4 * quad + 4, :].bitcast(I32)
             )
-        warm = sb.tile([P, 1], F32, name="warm")
-        warm_out = sb.tile([P, 1], F32, name="warm_out")
-        nc.vector.memset(warm[:], 0.0)
-        nc.scalar.activation(warm_out[:], warm[:], ACT.Exp)
-
-        qs = sb.tile([P, B * NQ], U8, name="qs", align_bytes=64)
+        qw = sb.tile([P, B * NQ], U32, name="qw", align_bytes=64)
+        nc.gpsimd.dma_start(
+            qw[:].bitcast(I32).rearrange("g (b q) -> g b q", b=B),
+            q_words[:, 0].rearrange("b g q r -> g b (q r)").bitcast(I32),
+        )
         ident = sb.tile([P, P], F32, name="ident")
-        make_identity(nc, ident[:])
-        nc.gpsimd.memset(qs[:].bitcast(I32), 0)
+        nc.vector.memset(ident[:], 0.0)
+        make_identity(nc, ident[:], nomemset=True)
+        qs = sb.tile([P, B * NQ], U8, name="qs", align_bytes=64)
+        nc.vector.memset(qs[:].bitcast(I32), 0)
         for quad in range(4):
             nc.gpsimd.dma_start(
                 qs[32 * quad : 32 * quad + 4, :].bitcast(I32).rearrange("r (b w) -> r b w", b=B),
                 q_scales[:, 0, 4 * quad : 4 * quad + 4, :].bitcast(I32).rearrange("b r w -> r b w"),
             )
+        vs_pool = sb.tile([P, T], F32, name="vs_pool", tag="v3")
+        nc.vector.memset(vs_pool[:], 0.0)
+        nc.scalar.dma_start(vs_pool[0:1, :], vs[0:1, :])
 
-        vs_got = sb.tile([P, B * N], F32, name="vs_got")
-        nc.vector.tensor_copy(vs_got[:], vs_pool[:].indirect(offsets[:]))
         ks_got = sb.tile([P, B * N], U8, name="ks_got", align_bytes=64)
         nc.vector.tensor_copy(ks_got[:], ks_pool[:].indirect(offsets[:]))
+        vs_got = sb.tile([P, B * N], F32, name="vs_got")
+        nc.vector.tensor_copy(vs_got[:], vs_pool[:].indirect(offsets[:]))
         v_pool[2] = load_values(2, "v2")
         v_pool[3] = load_values(3, "v3")
 
@@ -111,7 +107,7 @@ def tile_attend_qpk_kernel(tc, q_words, q_scales, k_words, k_scales, vT, vs, off
         w_codes, w_scales, inv_sum = [], [], []
         for b in range(B):
             q_cols = slice(b * NQ, (b + 1) * NQ)
-            score = ps.tile([NQ, N], F32, name=f"score{b}")
+            score = ps.tile([NQ, N], F32, name=f"score{b}", tag=f"score{b}")
             nc.tensor.matmul_mx(
                 out=score[:],
                 lhsT=qw[:, q_cols].bitcast(FP8X4),
@@ -146,8 +142,13 @@ def tile_attend_qpk_kernel(tc, q_words, q_scales, k_words, k_scales, vT, vs, off
                 out=w_codes[b][:].bitcast(FP8X4), scales=w_scales[b][:], in_=weight[:].rearrange("s q t -> s (q t)")
             )
 
-        acc = [ps.tile([NQ, DV], F32, name=f"acc{b}") for b in range(B)]
-        result = {}
+        acc_first = [ps.tile([NQ, DV - P], F32, name=f"acc_first{b}") for b in range(B)]
+        acc_last = [ps.tile([NQ, P], F32, name=f"acc_last{b}", tag=f"score{b}") for b in range(B)]
+
+        def acc(b, first, last):
+            if first == BLOCKS - 1:
+                return acc_last[b][:]
+            return acc_first[b][:, first * P : last * P]
 
         def multiply(j, got, seqs, name, bank):
             count = len(seqs)
@@ -164,10 +165,9 @@ def tile_attend_qpk_kernel(tc, q_words, q_scales, k_words, k_scales, vT, vs, off
             codes = sb.tile([P, count * P], U32, name=f"v_codes{name}", align_bytes=64)
             scales = sb.tile([P, count * P], U8, name=f"v_scales{name}", align_bytes=64)
             nc.vector.quantize_mx(out=codes[:].bitcast(FP8X4), scales=scales[:], in_=woven[:])
-            e_cols = slice(j * P, (j + 1) * P)
             for i, b in enumerate(seqs):
                 nc.tensor.matmul_mx(
-                    out=acc[b][:, e_cols],
+                    out=acc(b, j, j + 1),
                     lhsT=w_codes[b][:].bitcast(FP8X4),
                     lhsT_scale=w_scales[b][:],
                     rhs=codes[:, i * P : (i + 1) * P].bitcast(FP8X4),
@@ -179,7 +179,7 @@ def tile_attend_qpk_kernel(tc, q_words, q_scales, k_words, k_scales, vT, vs, off
         def store(b, first, last):
             cols = slice(first * P, last * P)
             staged = sb.tile([NQ, (last - first) * P], F32, name=f"staged{b}_{first}")
-            nc.scalar.activation(staged[:], acc[b][:, cols], ACT.Copy, scale=inv_sum[b][:])
+            nc.scalar.activation(staged[:], acc(b, first, last), ACT.Copy, scale=inv_sum[b][:])
             nc.sync.dma_start(out[b, :, cols], staged[:])
 
         for j in range(BLOCKS - 1):

@@ -6,8 +6,8 @@ from concourse.masks import make_identity
 B, N, T, D, DV, NQ = 2, 512, 2048, 512, 512, 128
 P = 128
 PACK = 4
-BLOCKS = DV // P
-SCALAR_BLOCKS = 2
+QUADRANTS = 4
+HALF = DV // 2
 
 FLOPS = 2 * B * NQ * N * (D + DV)
 
@@ -22,12 +22,35 @@ ACT = mybir.ActivationFunctionType
 ALU = mybir.AluOpType
 AXIS = mybir.AxisListType
 
+KIB = 1024
+SLOT = 64
+V2_AT = 0
+VS_POOL_AT = 4 * KIB
+QS_AT = 8 * KIB
+V3_AT = 12 * KIB
+KS_POOL_AT = 19 * KIB
+CAST0_AT = 22 * KIB
+V1_AT = 26 * KIB
+NEG_MAX_AT = V1_AT
+VS_COL_AT = CAST0_AT
+W_PLANES_AT = V3_AT
+INV_SUM_AT = V3_AT + 2 * KIB
+V_PLANES_AT = V3_AT + 2 * KIB + 4 * SLOT
+V_PLANES_BYTES = B * P * (4 + 1)
+
 
 def tile_attend_qpk_kernel(tc, q_words, q_scales, k_words, k_scales, vT, vs, offs, out):
     nc = tc.nc
     with ExitStack() as ctx:
         sb = ctx.enter_context(tc.tile_pool(name="sb", bufs=1))
+        shared = ctx.enter_context(tc.tile_pool(name="shared", bufs=1))
         ps = ctx.enter_context(tc.psum_pool(name="ps", bufs=1))
+
+        def placed(shape, dtype, name, offset):
+            return shared.tile(shape, dtype, name=name, offset=offset, align_bytes=SLOT)
+
+        ident = sb.tile([P, P], F32, name="ident")
+        make_identity(nc, ident[:])
 
         offsets = sb.tile([P, B * N // 16], U16, name="offsets")
         nc.sync.dma_start(offsets[:], offs)
@@ -35,81 +58,65 @@ def tile_attend_qpk_kernel(tc, q_words, q_scales, k_words, k_scales, vT, vs, off
         def seq_offsets(b):
             return offsets[:, b * (N // 16) : (b + 1) * (N // 16)]
 
-        def load_values(j, tag):
-            pool_tile = sb.tile([P, T], F32, name=f"v_pool{j}", tag=tag)
+        def load_values(j, pool_tile):
             nc.sync.dma_start(pool_tile[:], vT[j * P : (j + 1) * P, :])
             return pool_tile
 
-        v_pool = {0: load_values(0, "v0")}
         kw_pool = sb.tile([P, T], U32, name="kw_pool")
         nc.sync.dma_start(kw_pool[:].bitcast(I32), k_words[0].rearrange("g t r -> g (t r)").bitcast(I32))
-        v_pool[1] = load_values(1, "v1")
+        v_pool0 = load_values(0, sb.tile([P, T], F32, name="v_pool0"))
+        v_pool1 = load_values(1, placed([P, T], F32, "v_pool1", V1_AT))
 
-        ks_pool = sb.tile([P, T], U8, name="ks_pool", tag="v2")
-        nc.vector.memset(ks_pool[:].bitcast(I32), 0)
-        for quad in range(4):
-            nc.scalar.dma_start(
-                ks_pool[32 * quad : 32 * quad + 4, :].bitcast(I32), k_scales[0, 4 * quad : 4 * quad + 4, :].bitcast(I32)
-            )
-        qw = sb.tile([P, B * NQ], U32, name="qw", align_bytes=64)
-        nc.gpsimd.dma_start(
+        qw = sb.tile([P, B * NQ], U32, name="qw", align_bytes=SLOT)
+        nc.scalar.dma_start(
             qw[:].bitcast(I32).rearrange("g (b q) -> g b q", b=B),
             q_words[:, 0].rearrange("b g q r -> g b (q r)").bitcast(I32),
         )
-        ident = sb.tile([P, P], F32, name="ident")
-        nc.vector.memset(ident[:], 0.0)
-        make_identity(nc, ident[:], nomemset=True)
-        qs = sb.tile([P, B * NQ], U8, name="qs", align_bytes=64)
-        nc.vector.memset(qs[:].bitcast(I32), 0)
-        for quad in range(4):
-            nc.gpsimd.dma_start(
-                qs[32 * quad : 32 * quad + 4, :].bitcast(I32).rearrange("r (b w) -> r b w", b=B),
-                q_scales[:, 0, 4 * quad : 4 * quad + 4, :].bitcast(I32).rearrange("b r w -> r b w"),
-            )
-        vs_pool = sb.tile([P, T], F32, name="vs_pool", tag="v3")
+        vs_pool = placed([P, T], F32, "vs_pool", VS_POOL_AT)
         nc.vector.memset(vs_pool[:], 0.0)
         nc.scalar.dma_start(vs_pool[0:1, :], vs[0:1, :])
-
-        ks_got = sb.tile([P, B * N], U8, name="ks_got", align_bytes=64)
-        nc.vector.tensor_copy(ks_got[:], ks_pool[:].indirect(offsets[:]))
-        vs_got = sb.tile([P, B * N], F32, name="vs_got")
-        nc.vector.tensor_copy(vs_got[:], vs_pool[:].indirect(offsets[:]))
-        v_pool[2] = load_values(2, "v2")
-        v_pool[3] = load_values(3, "v3")
-
-        def scalar_gather(j):
-            cast = sb.tile([P, T], BF16, name=f"v_cast{j}")
-            nc.scalar.activation(cast[:], v_pool[j][:], ACT.Copy)
-            got = sb.tile([P, B * N], BF16, name=f"v_got{j}")
-            nc.scalar.activation(got[:], cast[:].indirect(offsets[:]), ACT.Copy)
-            return got
-
-        def vector_gather(j, offsets_used, seqs, name):
-            got = sb.tile([P, seqs * N], BF16, name=name)
-            nc.vector.tensor_copy(got[:], v_pool[j][:].indirect(offsets_used))
-            return got
+        ks_pool = placed([P, T], U8, "ks_pool", KS_POOL_AT)
+        nc.vector.memset(ks_pool[:].bitcast(I32), 0)
+        for quad in range(QUADRANTS):
+            nc.scalar.dma_start(
+                ks_pool[32 * quad : 32 * quad + 4, :].bitcast(I32), k_scales[0, 4 * quad : 4 * quad + 4, :].bitcast(I32)
+            )
 
         kw_got = []
         for b in range(B):
-            kw_got.append(sb.tile([P, N], U32, name=f"kw_got{b}", align_bytes=64))
+            kw_got.append(sb.tile([P, N], U32, name=f"kw_got{b}", align_bytes=SLOT))
             nc.vector.tensor_copy(kw_got[b][:], kw_pool[:].indirect(seq_offsets(b)))
+        vs_got = sb.tile([P, B * N], F32, name="vs_got")
+        nc.vector.tensor_copy(vs_got[:], vs_pool[:].indirect(offsets[:]))
+        qs = placed([P, B * NQ], U8, "qs", QS_AT)
+        for quad in range(QUADRANTS):
+            nc.sync.dma_start(
+                qs[32 * quad : 32 * quad + 4, :].bitcast(I32).rearrange("r (b w) -> r b w", b=B),
+                q_scales[:, 0, 4 * quad : 4 * quad + 4, :].bitcast(I32).rearrange("b r w -> r b w"),
+            )
+        v_pool2 = load_values(2, placed([P, T], F32, "v_pool2", V2_AT))
+        ks_got = sb.tile([P, B * N], U8, name="ks_got", align_bytes=SLOT)
+        nc.vector.tensor_copy(ks_got[:], ks_pool[:].indirect(offsets[:]))
+        v_pool3 = load_values(3, placed([P, T], F32, "v_pool3", V3_AT))
 
-        vs_col = []
-        for b in range(B):
-            turned = ps.tile([P, PACK, P], F32, name=f"vs_turned{b}", tag=f"turn{b}")
-            for t in range(PACK):
-                nc.tensor.transpose(turned[:, t, :], vs_got[:, b * N + t : (b + 1) * N : PACK], ident[:])
-            vs_col.append(sb.tile([P, PACK], F32, name=f"vs_col{b}"))
-            nc.scalar.copy(vs_col[b][:], turned[:, :, 0])
+        v_cast0 = placed([P, T], BF16, "v_cast0", CAST0_AT)
+        nc.scalar.activation(v_cast0[:], v_pool0[:], ACT.Copy)
+        v_got0 = sb.tile([P, B * N], BF16, name="v_got0")
+        nc.scalar.activation(v_got0[:], v_cast0[:].indirect(offsets[:]), ACT.Copy)
 
-        got0 = scalar_gather(0) if SCALAR_BLOCKS > 0 else None
+        def vector_gather(pool_tile, offsets_used, seq_count, name):
+            got = sb.tile([P, seq_count * N], BF16, name=name)
+            nc.vector.tensor_copy(got[:], pool_tile[:].indirect(offsets_used))
+            return got
 
-        w_codes, w_scales, inv_sum = [], [], []
+        v_got1 = vector_gather(v_pool1, offsets[:], B, "v_got1")
+
+        score, neg_max = [], []
         for b in range(B):
             q_cols = slice(b * NQ, (b + 1) * NQ)
-            score = ps.tile([NQ, N], F32, name=f"score{b}", tag=f"score{b}")
+            score.append(ps.tile([NQ, N], F32, name=f"score{b}", tag=f"score{b}"))
             nc.tensor.matmul_mx(
-                out=score[:],
+                out=score[b][:],
                 lhsT=qw[:, q_cols].bitcast(FP8X4),
                 lhsT_scale=qs[:, q_cols],
                 rhs=kw_got[b][:].bitcast(FP8X4),
@@ -117,57 +124,81 @@ def tile_attend_qpk_kernel(tc, q_words, q_scales, k_words, k_scales, vT, vs, off
                 start=True,
                 stop=True,
             )
-            neg_max = sb.tile([NQ, 1], F32, name=f"neg_max{b}")
-            nc.vector.tensor_reduce(neg_max[:], score[:], AXIS.X, ALU.max, negate=True)
-            prob = sb.tile([NQ, PACK, P], F32, name=f"prob{b}")
-            row_sum = sb.tile([NQ, 1], F32, name=f"row_sum{b}")
-            nc.scalar.activation(
-                prob[:], score[:].rearrange("q (s t) -> q t s", t=PACK), ACT.Exp, bias=neg_max[:], accum_out=row_sum[:]
-            )
-            prob_turned = ps.tile([P, PACK, NQ], F32, name=f"prob_turned{b}", tag=f"turn{b}")
+            neg_max.append(placed([NQ, 1], F32, f"neg_max{b}", NEG_MAX_AT + SLOT * b))
+            nc.vector.tensor_reduce(neg_max[b][:], score[b][:], AXIS.X, ALU.max, negate=True)
+
+        vs_col = []
+        for b in range(B):
+            vs_turned = ps.tile([P, PACK, P], F32, name=f"vs_turned{b}", tag=f"turn{b}")
             for t in range(PACK):
-                nc.tensor.transpose(prob_turned[:, t, :], prob[:, t, :], ident[:])
-            weight = sb.tile([P, NQ, PACK], BF16, name=f"weight{b}", align_bytes=64)
-            nc.vector.tensor_tensor(
-                weight[:],
-                prob_turned[:].rearrange("s t q -> s q t"),
-                vs_col[b][:].unsqueeze(1).broadcast_to([P, NQ, PACK]),
-                ALU.mult,
-            )
-            inv_sum.append(sb.tile([NQ, 1], F32, name=f"inv_sum{b}"))
-            nc.vector.reciprocal(inv_sum[b][:], row_sum[:])
-            w_codes.append(sb.tile([P, NQ], U32, name=f"w_codes{b}", align_bytes=64))
-            w_scales.append(sb.tile([P, NQ], U8, name=f"w_scales{b}", align_bytes=64))
-            nc.vector.quantize_mx(
-                out=w_codes[b][:].bitcast(FP8X4), scales=w_scales[b][:], in_=weight[:].rearrange("s q t -> s (q t)")
-            )
+                nc.tensor.transpose(vs_turned[:, t, :], vs_got[:, b * N + t : (b + 1) * N : PACK], ident[:])
+            vs_col.append(placed([P, PACK], F32, f"vs_col{b}", VS_COL_AT + SLOT * b))
+            nc.scalar.copy(vs_col[b][:], vs_turned[:, :, 0])
 
-        acc_first = [ps.tile([NQ, DV - P], F32, name=f"acc_first{b}") for b in range(B)]
-        acc_last = [ps.tile([NQ, P], F32, name=f"acc_last{b}", tag=f"score{b}") for b in range(B)]
-
-        def acc(b, first, last):
-            if first == BLOCKS - 1:
-                return acc_last[b][:]
-            return acc_first[b][:, first * P : last * P]
-
-        def multiply(j, got, seqs, name, bank):
-            count = len(seqs)
-            words = got[:].bitcast(F32)
-            turned = ps.tile([P, count, 2, P], F32, name=f"v_turned{name}", tag=f"v_turn{bank}")
-            for i in range(count):
+        def turn_values(got, seq_count, name, bank):
+            pairs = got[:].bitcast(F32)
+            v_turned = ps.tile([P, seq_count, 2, P], F32, name=f"v_turned{name}", tag=bank)
+            for i in range(seq_count):
                 for u in range(2):
-                    nc.tensor.transpose(turned[:, i, u, :], words[:, i * (N // 2) + u : (i + 1) * (N // 2) : 2], ident[:])
-            woven = sb.tile([P, count * P * PACK], BF16, name=f"v_woven{name}", align_bytes=64)
+                    nc.tensor.transpose(
+                        v_turned[:, i, u, :], pairs[:, i * (N // 2) + u : (i + 1) * (N // 2) : 2], ident[:]
+                    )
+            woven = sb.tile([P, seq_count * P * PACK], BF16, name=f"v_woven{name}", align_bytes=SLOT)
             nc.scalar.copy(
-                woven[:].bitcast(F32).rearrange("s (i e u) -> s i e u", i=count, u=2),
-                turned[:].rearrange("s i u e -> s i e u"),
+                woven[:].bitcast(F32).rearrange("s (i e u) -> s i e u", i=seq_count, u=2),
+                v_turned[:].rearrange("s i u e -> s i e u"),
             )
-            codes = sb.tile([P, count * P], U32, name=f"v_codes{name}", align_bytes=64)
-            scales = sb.tile([P, count * P], U8, name=f"v_scales{name}", align_bytes=64)
+            return woven
+
+        woven0 = turn_values(v_got0, B, "0", "v_turn1")
+
+        prob_turned, row_sum = [], []
+        for b in range(B):
+            prob = sb.tile([NQ, PACK, P], F32, name=f"prob{b}")
+            row_sum.append(sb.tile([NQ, 1], F32, name=f"row_sum{b}"))
+            nc.scalar.activation(
+                prob[:],
+                score[b][:].rearrange("q (s t) -> q t s", t=PACK),
+                ACT.Exp,
+                bias=neg_max[b][:],
+                accum_out=row_sum[b][:],
+            )
+            prob_turned.append(ps.tile([P, PACK, NQ], F32, name=f"prob_turned{b}", tag=f"turn{b}"))
+            for t in range(PACK):
+                nc.tensor.transpose(prob_turned[b][:, t, :], prob[:, t, :], ident[:])
+
+        v_got2 = vector_gather(v_pool2, offsets[:], B, "v_got2")
+        v_got3 = [vector_gather(v_pool3, seq_offsets(b), 1, f"v_got3_{b}") for b in range(B)]
+
+        weight = []
+        for b in range(B):
+            product = sb.tile([P, PACK, NQ], F32, name=f"product{b}")
+            for t in range(PACK):
+                nc.scalar.activation(product[:, t, :], prob_turned[b][:, t, :], ACT.Copy, scale=vs_col[b][:, t : t + 1])
+            weight.append(sb.tile([P, NQ, PACK], BF16, name=f"weight{b}", align_bytes=SLOT))
+            nc.scalar.copy(weight[b][:], product[:].rearrange("s t q -> s q t"))
+        w_codes, w_scales, inv_sum = [], [], []
+        for b in range(B):
+            w_codes.append(placed([P, NQ], U32, f"w_codes{b}", W_PLANES_AT + b * KIB))
+            w_scales.append(placed([P, NQ], U8, f"w_scales{b}", W_PLANES_AT + b * KIB + NQ * 4))
+            nc.vector.quantize_mx(
+                out=w_codes[b][:].bitcast(FP8X4), scales=w_scales[b][:], in_=weight[b][:].rearrange("s q t -> s (q t)")
+            )
+            inv_sum.append(placed([NQ, 1], F32, f"inv_sum{b}", INV_SUM_AT + SLOT * b))
+            nc.vector.reciprocal(inv_sum[b][:], row_sum[b][:])
+
+        woven1 = turn_values(v_got1, B, "1", "score0")
+        woven2 = turn_values(v_got2, B, "2", "score1")
+        acc = [
+            [ps.tile([NQ, HALF], F32, name=f"acc_low{b}") for b in range(B)],
+            [ps.tile([NQ, HALF], F32, name=f"acc_high{b}", tag=f"score{b}") for b in range(B)],
+        ]
+
+        def multiply(j, woven, seqs, codes, scales):
             nc.vector.quantize_mx(out=codes[:].bitcast(FP8X4), scales=scales[:], in_=woven[:])
             for i, b in enumerate(seqs):
                 nc.tensor.matmul_mx(
-                    out=acc(b, j, j + 1),
+                    out=acc[j // 2][b][:, (j % 2) * P : (j % 2 + 1) * P],
                     lhsT=w_codes[b][:].bitcast(FP8X4),
                     lhsT_scale=w_scales[b][:],
                     rhs=codes[:, i * P : (i + 1) * P].bitcast(FP8X4),
@@ -176,23 +207,28 @@ def tile_attend_qpk_kernel(tc, q_words, q_scales, k_words, k_scales, vT, vs, off
                     stop=True,
                 )
 
-        def store(b, first, last):
-            cols = slice(first * P, last * P)
-            staged = sb.tile([NQ, (last - first) * P], F32, name=f"staged{b}_{first}")
-            nc.scalar.activation(staged[:], acc(b, first, last), ACT.Copy, scale=inv_sum[b][:])
-            nc.sync.dma_start(out[b, :, cols], staged[:])
+        def multiply_both(j, woven):
+            at = V_PLANES_AT + j * V_PLANES_BYTES
+            codes = placed([P, B * P], U32, f"v_codes{j}", at)
+            scales = placed([P, B * P], U8, f"v_scales{j}", at + B * P * 4)
+            multiply(j, woven, range(B), codes, scales)
 
-        for j in range(BLOCKS - 1):
-            if j == 0 and SCALAR_BLOCKS > 0:
-                got = got0
-            elif j < SCALAR_BLOCKS:
-                got = scalar_gather(j)
+        def store(half, b, on_vector):
+            staged = sb.tile([NQ, HALF], F32, name=f"staged{half}_{b}")
+            if on_vector:
+                nc.vector.tensor_scalar(staged[:], acc[half][b][:], inv_sum[b][:], None, ALU.mult)
             else:
-                got = vector_gather(j, offsets[:], B, f"v_got{j}")
-            multiply(j, got, list(range(B)), f"{j}", j % 2)
-        last_got = [vector_gather(BLOCKS - 1, seq_offsets(b), 1, f"v_got_last{b}") for b in range(B)]
+                nc.scalar.activation(staged[:], acc[half][b][:], ACT.Copy, scale=inv_sum[b][:])
+            nc.sync.dma_start(out[b, :, half * HALF : (half + 1) * HALF], staged[:])
+
+        multiply_both(0, woven0)
+        multiply_both(1, woven1)
+        woven3 = [turn_values(v_got3[b], 1, f"3_{b}", f"v_turn{b}") for b in range(B)]
         for b in range(B):
-            store(b, 0, BLOCKS - 1)
+            store(0, b, on_vector=False)
+        multiply_both(2, woven2)
         for b in range(B):
-            multiply(BLOCKS - 1, last_got[b], [b], f"last{b}", (BLOCKS - 1 + b) % 2)
-            store(b, BLOCKS - 1, BLOCKS)
+            codes3 = sb.tile([P, P], U32, name=f"v_codes3_{b}", align_bytes=SLOT)
+            scales3 = sb.tile([P, P], U8, name=f"v_scales3_{b}", align_bytes=SLOT)
+            multiply(3, woven3[b], [b], codes3, scales3)
+            store(1, b, on_vector=(b == B - 1))

from contextlib import ExitStack

import concourse.mybir as mybir
from concourse.masks import make_identity

B, N, T, D, DV, NQ = 2, 512, 2048, 512, 512, 128
P = 128
PACK = 4
QUADRANTS = 4
HALF = DV // 2

FLOPS = 2 * B * NQ * N * (D + DV)

F32 = mybir.dt.float32
BF16 = mybir.dt.bfloat16
I32 = mybir.dt.int32
U32 = mybir.dt.uint32
U16 = mybir.dt.uint16
U8 = mybir.dt.uint8
FP8X4 = mybir.dt.float8_e4m3fn_x4
ACT = mybir.ActivationFunctionType
ALU = mybir.AluOpType
AXIS = mybir.AxisListType

KIB = 1024
SLOT = 64
V2_AT = 0
VS_POOL_AT = 4 * KIB
QS_AT = 8 * KIB
V3_AT = 12 * KIB
KS_POOL_AT = 19 * KIB
CAST0_AT = 22 * KIB
V1_AT = 26 * KIB
NEG_MAX_AT = V1_AT
VS_COL_AT = CAST0_AT
W_PLANES_AT = V3_AT
INV_SUM_AT = V3_AT + 2 * KIB
V_PLANES_AT = V3_AT + 2 * KIB + 4 * SLOT
V_PLANES_BYTES = B * P * (4 + 1)


def tile_attend_qpk_kernel(tc, q_words, q_scales, k_words, k_scales, vT, vs, offs, out):
    nc = tc.nc
    with ExitStack() as ctx:
        sb = ctx.enter_context(tc.tile_pool(name="sb", bufs=1))
        shared = ctx.enter_context(tc.tile_pool(name="shared", bufs=1))
        ps = ctx.enter_context(tc.psum_pool(name="ps", bufs=1))

        def placed(shape, dtype, name, offset):
            return shared.tile(shape, dtype, name=name, offset=offset, align_bytes=SLOT)

        ident = sb.tile([P, P], F32, name="ident")
        make_identity(nc, ident[:])

        offsets = sb.tile([P, B * N // 16], U16, name="offsets")
        nc.sync.dma_start(offsets[:], offs)

        def seq_offsets(b):
            return offsets[:, b * (N // 16) : (b + 1) * (N // 16)]

        def load_values(j, pool_tile):
            nc.sync.dma_start(pool_tile[:], vT[j * P : (j + 1) * P, :])
            return pool_tile

        kw_pool = sb.tile([P, T], U32, name="kw_pool")
        nc.sync.dma_start(kw_pool[:].bitcast(I32), k_words[0].rearrange("g t r -> g (t r)").bitcast(I32))
        v_pool0 = load_values(0, sb.tile([P, T], F32, name="v_pool0"))
        v_pool1 = load_values(1, placed([P, T], F32, "v_pool1", V1_AT))

        qw = sb.tile([P, B * NQ], U32, name="qw", align_bytes=SLOT)
        nc.scalar.dma_start(
            qw[:].bitcast(I32).rearrange("g (b q) -> g b q", b=B),
            q_words[:, 0].rearrange("b g q r -> g b (q r)").bitcast(I32),
        )
        vs_pool = placed([P, T], F32, "vs_pool", VS_POOL_AT)
        nc.vector.memset(vs_pool[:], 0.0)
        nc.scalar.dma_start(vs_pool[0:1, :], vs[0:1, :])
        ks_pool = placed([P, T], U8, "ks_pool", KS_POOL_AT)
        nc.vector.memset(ks_pool[:].bitcast(I32), 0)
        for quad in range(QUADRANTS):
            nc.scalar.dma_start(
                ks_pool[32 * quad : 32 * quad + 4, :].bitcast(I32), k_scales[0, 4 * quad : 4 * quad + 4, :].bitcast(I32)
            )

        kw_got = []
        for b in range(B):
            kw_got.append(sb.tile([P, N], U32, name=f"kw_got{b}", align_bytes=SLOT))
            nc.vector.tensor_copy(kw_got[b][:], kw_pool[:].indirect(seq_offsets(b)))
        vs_got = sb.tile([P, B * N], F32, name="vs_got")
        nc.vector.tensor_copy(vs_got[:], vs_pool[:].indirect(offsets[:]))
        qs = placed([P, B * NQ], U8, "qs", QS_AT)
        for quad in range(QUADRANTS):
            nc.sync.dma_start(
                qs[32 * quad : 32 * quad + 4, :].bitcast(I32).rearrange("r (b w) -> r b w", b=B),
                q_scales[:, 0, 4 * quad : 4 * quad + 4, :].bitcast(I32).rearrange("b r w -> r b w"),
            )
        v_pool2 = load_values(2, placed([P, T], F32, "v_pool2", V2_AT))
        ks_got = sb.tile([P, B * N], U8, name="ks_got", align_bytes=SLOT)
        nc.vector.tensor_copy(ks_got[:], ks_pool[:].indirect(offsets[:]))
        v_pool3 = load_values(3, placed([P, T], F32, "v_pool3", V3_AT))

        v_cast0 = placed([P, T], BF16, "v_cast0", CAST0_AT)
        nc.scalar.activation(v_cast0[:], v_pool0[:], ACT.Copy)
        v_got0 = sb.tile([P, B * N], BF16, name="v_got0")
        nc.scalar.activation(v_got0[:], v_cast0[:].indirect(offsets[:]), ACT.Copy)

        def vector_gather(pool_tile, offsets_used, seq_count, name):
            got = sb.tile([P, seq_count * N], BF16, name=name)
            nc.vector.tensor_copy(got[:], pool_tile[:].indirect(offsets_used))
            return got

        v_got1 = vector_gather(v_pool1, offsets[:], B, "v_got1")

        score, neg_max = [], []
        for b in range(B):
            q_cols = slice(b * NQ, (b + 1) * NQ)
            score.append(ps.tile([NQ, N], F32, name=f"score{b}", tag=f"score{b}"))
            nc.tensor.matmul_mx(
                out=score[b][:],
                lhsT=qw[:, q_cols].bitcast(FP8X4),
                lhsT_scale=qs[:, q_cols],
                rhs=kw_got[b][:].bitcast(FP8X4),
                rhs_scale=ks_got[:, b * N : (b + 1) * N],
                start=True,
                stop=True,
            )
            neg_max.append(placed([NQ, 1], F32, f"neg_max{b}", NEG_MAX_AT + SLOT * b))
            nc.vector.tensor_reduce(neg_max[b][:], score[b][:], AXIS.X, ALU.max, negate=True)

        vs_col = []
        for b in range(B):
            vs_turned = ps.tile([P, PACK, P], F32, name=f"vs_turned{b}", tag=f"turn{b}")
            for t in range(PACK):
                nc.tensor.transpose(vs_turned[:, t, :], vs_got[:, b * N + t : (b + 1) * N : PACK], ident[:])
            vs_col.append(placed([P, PACK], F32, f"vs_col{b}", VS_COL_AT + SLOT * b))
            nc.scalar.copy(vs_col[b][:], vs_turned[:, :, 0])

        def turn_values(got, seq_count, name, bank):
            pairs = got[:].bitcast(F32)
            v_turned = ps.tile([P, seq_count, 2, P], F32, name=f"v_turned{name}", tag=bank)
            for i in range(seq_count):
                for u in range(2):
                    nc.tensor.transpose(
                        v_turned[:, i, u, :], pairs[:, i * (N // 2) + u : (i + 1) * (N // 2) : 2], ident[:]
                    )
            woven = sb.tile([P, seq_count * P * PACK], BF16, name=f"v_woven{name}", align_bytes=SLOT)
            nc.scalar.copy(
                woven[:].bitcast(F32).rearrange("s (i e u) -> s i e u", i=seq_count, u=2),
                v_turned[:].rearrange("s i u e -> s i e u"),
            )
            return woven

        woven0 = turn_values(v_got0, B, "0", "v_turn1")

        prob_turned, row_sum = [], []
        for b in range(B):
            prob = sb.tile([NQ, PACK, P], F32, name=f"prob{b}")
            row_sum.append(sb.tile([NQ, 1], F32, name=f"row_sum{b}"))
            nc.scalar.activation(
                prob[:],
                score[b][:].rearrange("q (s t) -> q t s", t=PACK),
                ACT.Exp,
                bias=neg_max[b][:],
                accum_out=row_sum[b][:],
            )
            prob_turned.append(ps.tile([P, PACK, NQ], F32, name=f"prob_turned{b}", tag=f"turn{b}"))
            for t in range(PACK):
                nc.tensor.transpose(prob_turned[b][:, t, :], prob[:, t, :], ident[:])

        v_got2 = vector_gather(v_pool2, offsets[:], B, "v_got2")
        v_got3 = [vector_gather(v_pool3, seq_offsets(b), 1, f"v_got3_{b}") for b in range(B)]

        weight = []
        for b in range(B):
            product = sb.tile([P, PACK, NQ], F32, name=f"product{b}")
            for t in range(PACK):
                nc.scalar.activation(product[:, t, :], prob_turned[b][:, t, :], ACT.Copy, scale=vs_col[b][:, t : t + 1])
            weight.append(sb.tile([P, NQ, PACK], BF16, name=f"weight{b}", align_bytes=SLOT))
            nc.scalar.copy(weight[b][:], product[:].rearrange("s t q -> s q t"))
        w_codes, w_scales, inv_sum = [], [], []
        for b in range(B):
            w_codes.append(placed([P, NQ], U32, f"w_codes{b}", W_PLANES_AT + b * KIB))
            w_scales.append(placed([P, NQ], U8, f"w_scales{b}", W_PLANES_AT + b * KIB + NQ * 4))
            nc.vector.quantize_mx(
                out=w_codes[b][:].bitcast(FP8X4), scales=w_scales[b][:], in_=weight[b][:].rearrange("s q t -> s (q t)")
            )
            inv_sum.append(placed([NQ, 1], F32, f"inv_sum{b}", INV_SUM_AT + SLOT * b))
            nc.vector.reciprocal(inv_sum[b][:], row_sum[b][:])

        woven1 = turn_values(v_got1, B, "1", "score0")
        woven2 = turn_values(v_got2, B, "2", "score1")
        acc = [
            [ps.tile([NQ, HALF], F32, name=f"acc_low{b}") for b in range(B)],
            [ps.tile([NQ, HALF], F32, name=f"acc_high{b}", tag=f"score{b}") for b in range(B)],
        ]

        def multiply(j, woven, seqs, codes, scales):
            nc.vector.quantize_mx(out=codes[:].bitcast(FP8X4), scales=scales[:], in_=woven[:])
            for i, b in enumerate(seqs):
                nc.tensor.matmul_mx(
                    out=acc[j // 2][b][:, (j % 2) * P : (j % 2 + 1) * P],
                    lhsT=w_codes[b][:].bitcast(FP8X4),
                    lhsT_scale=w_scales[b][:],
                    rhs=codes[:, i * P : (i + 1) * P].bitcast(FP8X4),
                    rhs_scale=scales[:, i * P : (i + 1) * P],
                    start=True,
                    stop=True,
                )

        def multiply_both(j, woven):
            at = V_PLANES_AT + j * V_PLANES_BYTES
            codes = placed([P, B * P], U32, f"v_codes{j}", at)
            scales = placed([P, B * P], U8, f"v_scales{j}", at + B * P * 4)
            multiply(j, woven, range(B), codes, scales)

        def store(half, b, on_vector):
            staged = sb.tile([NQ, HALF], F32, name=f"staged{half}_{b}")
            if on_vector:
                nc.vector.tensor_scalar(staged[:], acc[half][b][:], inv_sum[b][:], None, ALU.mult)
            else:
                nc.scalar.activation(staged[:], acc[half][b][:], ACT.Copy, scale=inv_sum[b][:])
            nc.sync.dma_start(out[b, :, half * HALF : (half + 1) * HALF], staged[:])

        multiply_both(0, woven0)
        multiply_both(1, woven1)
        woven3 = [turn_values(v_got3[b], 1, f"3_{b}", f"v_turn{b}") for b in range(B)]
        for b in range(B):
            store(0, b, on_vector=False)
        multiply_both(2, woven2)
        for b in range(B):
            codes3 = sb.tile([P, P], U32, name=f"v_codes3_{b}", align_bytes=SLOT)
            scales3 = sb.tile([P, P], U8, name=f"v_scales3_{b}", align_bytes=SLOT)
            multiply(3, woven3[b], [b], codes3, scales3)
            store(1, b, on_vector=(b == B - 1))
